import numpy as np
import ml_dtypes


def mxq(x, axis, fmt="e4m3"):
    dtype, down = {"e4m3": (ml_dtypes.float8_e4m3fn, 7), "e5m2": (ml_dtypes.float8_e5m2, 14)}[fmt]
    v = np.moveaxis(np.asarray(x, np.float32).astype(ml_dtypes.bfloat16).astype(np.float64), axis, -1)
    blocks = v.reshape(v.shape[:-1] + (-1, 32))
    amax = np.abs(blocks).max(-1, keepdims=True)
    byte = np.maximum(np.where(amax > 0, np.frexp(amax)[1] - 1 + 127, 0) - down, 1)
    scale = np.exp2(byte - 127.0)
    codes = (blocks / scale).astype(np.float32).astype(dtype).astype(np.float64)
    return np.moveaxis((codes * scale).reshape(v.shape), -1, axis)


WIDE = False


def mx_kscale(k):
    if not WIDE:
        return np.ones(k)
    levels = np.array([10, -10, 5, -5, 0])
    if k % 512:
        return np.exp2(np.random.permutation(np.resize(levels, k // 32))).repeat(32)
    a = np.empty((k // 512, 16))
    for p in range(k // 512):
        a[p, :8] = np.random.permutation(np.resize(levels, 8))
        for g in range(8):
            far = levels[np.abs(levels - a[p, g]) >= 10]
            a[p, g + 8] = far[np.random.randint(len(far))]
    return np.exp2(a.ravel()).repeat(32)


def f64(x):
    return np.asarray(x).astype(np.float64)


def striped(idx):
    return np.tile(np.asarray(idx).reshape(-1, 16).T, (8, 1)).astype(np.uint16)


def unstriped(offs):
    return offs[:16].T.reshape(-1).astype(np.int64)


E2M1 = np.array([0.0, 0.5, 1.0, 1.5, 2.0, 3.0, 4.0, 6.0, -0.0, -0.5, -1.0, -1.5, -2.0, -3.0, -4.0, -6.0])


def pack_weight(w, fmt):
    k, n = w.shape
    w = f64(np.asarray(w, np.float32).astype(ml_dtypes.bfloat16)).reshape(k // 32, 32, n)
    amax = np.abs(w).max(1)
    if fmt == "e4m3":
        byte = np.frexp(amax)[1] - 1 + 127 - 7
    else:
        mant, ex = np.frexp(amax / 6.0)
        byte = np.where(mant > 0.5, ex, ex - 1) + 127
    byte = np.clip(np.where(amax > 0, byte, 1), 1, 254)
    scaled = (w * np.exp2(127.0 - byte)[:, None, :]).reshape(k, n).astype(np.float32)
    by_word = np.ascontiguousarray(scaled.reshape(k // 512, 128, 4, n).transpose(0, 1, 3, 2))
    if fmt == "e4m3":
        words = by_word.astype(ml_dtypes.float8_e4m3fn).view(np.uint8)
    else:
        c = by_word.astype(ml_dtypes.float4_e2m1fn).view(np.uint8) & 0xF
        words = (c[..., 0::2] | (c[..., 1::2] << 4)).reshape(k // 512, 128, 2 * n)
    return np.ascontiguousarray(words), np.ascontiguousarray(byte.astype(np.uint8).reshape(k // 512, 16, n))


def unpack_weight(words, scales, fmt):
    g, _, n = scales.shape
    words = np.ascontiguousarray(words).reshape(g, 128, n, -1)
    if fmt == "e4m3":
        vals = words.view(ml_dtypes.float8_e4m3fn).astype(np.float64)
    else:
        nib = np.empty((g, 128, n, 4), np.uint8)
        nib[..., 0::2] = words & 0xF
        nib[..., 1::2] = words >> 4
        vals = E2M1[nib]
    vals = vals * np.repeat(np.exp2(scales.astype(np.float64) - 127.0), 8, axis=1)[..., None]
    return vals.transpose(0, 1, 3, 2).reshape(g * 512, n)


def bf(x):
    return np.asarray(x, np.float32).astype(ml_dtypes.bfloat16)


def planes(Y):
    r, m = Y.shape
    b = f64(bf(Y)).reshape(r // 32, 32, m)
    amax = np.abs(b).max(1)
    byte = np.clip(np.where(amax > 0, np.frexp(amax)[1] - 1 + 127 - 7, 1), 1, 254)
    codes = (b * np.exp2(127.0 - byte)[:, None, :]).reshape(r, m).astype(np.float32).astype(ml_dtypes.float8_e4m3fn).view(np.uint8)
    words = codes.reshape(r // 512, 128, 4, m).transpose(0, 1, 3, 2)
    return np.ascontiguousarray(words), np.ascontiguousarray(byte.astype(np.uint8).reshape(r // 512, 16, m))


D, T, I, Q, E, Z, C = 512, 2048, 512, 512, 512, 1024, 256


def setup_inputs():
    n = np.random.standard_normal
    idx = np.random.permutation(T)[:I]
    idx2 = np.random.permutation(Z)[:I]
    idx3 = np.random.permutation(Q)[:C]
    fd = mx_kscale(D)
    fi = mx_kscale(I)
    ti = np.ones(T)
    ti[idx] = fi
    keysp = pack_weight(n((D, T)) / fd[:, None], "e2m1")
    return {
        "query": (n((D, Q)) * 1.0 / np.sqrt(D) * fd[:, None]).astype(np.float32),
        "keys_words": keysp[0],
        "keys_scales": keysp[1],
        "earl": (np.random.uniform(0.3, 1.7, (Q, Z))).astype(np.float32),
        "os": (np.random.uniform(0.02, 0.08, (1, I)) * fi).astype(np.float32),
        "vals": (n((E, T)) / ti).astype(np.float32),
        "pgain": (np.random.uniform(0.5, 2.0, (1, C))).astype(np.float32),
        "offs": striped(idx),
        "offs2": striped(idx2),
        "offs3": striped(idx3),
    }


def reference(query, keys_words, keys_scales, earl, os, vals, pgain, offs, offs2, offs3):
    idx = unstriped(offs)
    idx2 = unstriped(offs2)
    idx3 = unstriped(offs3)
    keysu = unpack_weight(keys_words, keys_scales, "e2m1")
    queryq = mxq(f64(query), 0, "e4m3")
    keysidxg = keysu[:, idx]
    a = queryq.T @ keysidxg
    w = a * f64(earl)[:, idx2]
    wo1 = w * f64(os)
    wt1 = wo1.T
    vt1 = f64(vals)[:, idx].T
    vt1q = mxq(vt1, 0, "e4m3")
    wt1q = mxq(wt1, 0, "e4m3")
    o = vt1q.T @ wt1q
    y = o[:, idx3] * f64(pgain)
    words, scales = planes(y)
    return y, words, scales

@@ -1,0 +1,254 @@
+from contextlib import ExitStack
+
+import concourse.mybir as mybir
+from concourse.masks import make_identity
+
+D, T, I, Q, E, Z, C = 512, 2048, 512, 512, 512, 1024, 256
+FLOPS = 2 * D * Q * I + 2 * I * E * Q
+
+F32 = mybir.dt.float32
+BF16 = mybir.dt.bfloat16
+I32 = mybir.dt.int32
+U32 = mybir.dt.uint32
+U16 = mybir.dt.uint16
+U8 = mybir.dt.uint8
+FP8X4 = mybir.dt.float8_e4m3fn_x4
+FP4X4 = mybir.dt.float4_e2m1fn_x4
+MULT = mybir.AluOpType.mult
+COPY = mybir.ActivationFunctionType.Copy
+
+P = 128
+PACK = 4
+SCALAR_SLOTS = 192
+
+
+def tile_attend_earliertable_pickedout_lean_pl_kernel(
+    tc, query, keys_words, keys_scales, earl, slot_factor, vals, pgain, offs, offs2, offs3, out_0, out_1, out_2
+):
+    nc = tc.nc
+    with ExitStack() as ctx:
+        keep = ctx.enter_context(tc.tile_pool(name="keep", bufs=1))
+        late = ctx.enter_context(tc.tile_pool(name="late", bufs=1))
+        psum = ctx.enter_context(tc.psum_pool(name="psum", bufs=1))
+
+        key_list = keep.tile([P, I // 16], U16, name="key_list")
+        earl_list = keep.tile([P, I // 16], U16, name="earl_list")
+        out_list = keep.tile([P, C // 16], U16, name="out_list")
+        key_words = keep.tile([P, T], U16, name="key_words")
+        key_bytes = keep.tile([P, T], U8, name="key_bytes")
+        query_raw = keep.tile([P, PACK, Q], F32, name="query_raw", tag="query")
+        os_cols = keep.tile([P, I // P], F32, name="os_cols")
+        gain_cols = keep.tile([P, C // P], F32, name="gain_cols")
+        earl_raw = [keep.tile([P, Z], F32, name="earl_raw%d" % j, tag="earl%d" % j, align_bytes=64) for j in range(Q // P)]
+        vals_raw = [keep.tile([P, T], F32, name="vals_raw%d" % r, tag="vals%d" % r, align_bytes=64) for r in range(PACK - 1)]
+        vals_raw.append(late.tile([P, T], F32, name="vals_raw3", align_bytes=64, offset=0))
+        ident = keep.tile([P, P], F32, name="ident")
+
+        nc.gpsimd.memset(key_bytes[:].bitcast(I32), 0)
+        vals_dealt = vals.rearrange("(p r) t -> r p t", r=PACK)
+        nc.sync.dma_start(key_words[:].bitcast(I32), keys_words[0].bitcast(I32))
+        nc.sync.dma_start(key_list[:], offs)
+        nc.sync.dma_start(os_cols[:], slot_factor.rearrange("o (n m) -> (o n) m", n=P))
+        nc.sync.dma_start(earl_list[:], offs2)
+        nc.sync.dma_start(earl_raw[0][:], earl[0:P, :])
+        nc.sync.dma_start(query_raw[:], query.rearrange("(p t) q -> p t q", t=PACK))
+        for quad in range(4):
+            nc.sync.dma_start(
+                key_bytes[32 * quad : 32 * quad + 4, :].bitcast(I32),
+                keys_scales[0][4 * quad : 4 * quad + 4, :].bitcast(I32),
+            )
+        for j in range(1, Q // P):
+            nc.sync.dma_start(earl_raw[j][:], earl[j * P : (j + 1) * P, :])
+        nc.sync.dma_start(vals_raw[0][:], vals_dealt[0])
+        nc.sync.dma_start(gain_cols[:], pgain.rearrange("o (n m) -> (o n) m", n=P))
+        nc.sync.dma_start(out_list[:], offs3)
+        for r in range(1, PACK):
+            nc.sync.dma_start(vals_raw[r][:], vals_dealt[r])
+
+        make_identity(nc, ident[:])
+
+        def spread(cols, width, name):
+            per = width // P
+            bank = psum.tile([P, per, P], F32, name=name + "_bank", tag="turn", bufs=4)
+            for m in range(per):
+                nc.tensor.transpose(bank[:, m, :], cols[:, m : m + 1].to_broadcast([P, P]), ident[:])
+            rows = keep.tile([P, width], F32, name=name)
+            nc.scalar.copy(rows[:].rearrange("p (n m) -> p n m", m=per), bank[:].rearrange("p m n -> p n m"))
+            return rows
+
+        def turn(src, dst):
+            words = src[:].bitcast(F32)
+            bank = psum.tile([P, 2, P], F32, name="turn_bank", tag="turn", bufs=4)
+            for u in range(2):
+                nc.tensor.transpose(bank[:, u, :], words[:, u : 2 * P : 2], ident[:])
+            nc.scalar.copy(
+                dst.bitcast(F32).rearrange("p (x u) -> p x u", u=2), bank[:].rearrange("p u x -> p x u")
+            )
+
+        half = Q // 2
+        picked_words = keep.tile([P, I], U16, name="picked_words", align_bytes=64)
+        picked_bytes = keep.tile([P, I], U8, name="picked_bytes", align_bytes=64)
+        q_codes = keep.tile([P, Q], U32, name="q_codes", align_bytes=64)
+        q_scales = keep.tile([P, Q], U8, name="q_scales", align_bytes=64)
+        w_codes, w_scales = {}, {}
+        out_dealt = out_0.rearrange("(p r) c -> p r c", r=PACK)
+        factor, w_bf, w_turned, v_bf, v_turned, v_codes, v_scales, o_whole = {}, {}, {}, {}, {}, {}, {}, {}
+
+        def pick_factor(j):
+            factor[j] = keep.tile([P, I], F32, name="factor%d" % j, tag="factor%d" % j, align_bytes=64)
+            if j > 0:
+                picked = keep.tile([P, I], F32, name="earl_picked%d" % j, tag=("", "query", "picked2", "picked3")[j])
+                nc.scalar.activation(picked[:], earl_raw[j][:].indirect(earl_list[:]), COPY)
+                nc.vector.tensor_tensor(factor[j][:], picked[:], os_rows[:], MULT)
+            else:
+                nc.vector.tensor_tensor(factor[j][:], earl_raw[j][:].indirect(earl_list[:]), os_rows[:], MULT)
+
+        def weigh(j):
+            cols = slice(j * P, (j + 1) * P)
+            score = psum.tile([P, I], F32, name="score", tag="product", bufs=4)
+            nc.tensor.matmul_mx(
+                score[:],
+                lhsT=q_codes[:, cols].bitcast(FP8X4),
+                lhsT_scale=q_scales[:, cols],
+                rhs=picked_words[:].bitcast(FP4X4),
+                rhs_scale=picked_bytes[:],
+                start=True,
+                stop=True,
+            )
+            w_bf[j] = keep.tile([P, I], BF16, name="w_bf%d" % j, tag="w_bf%d" % j, align_bytes=64)
+            nc.vector.tensor_tensor(w_bf[j][:], score[:], factor[j][:], MULT)
+
+        def turn_w(j):
+            tag = ("earl3", "w_turned1", "vals0", "w_turned3")[j]
+            w_turned[j] = keep.tile([P, P * PACK], BF16, name="w_turned%d" % j, tag=tag, align_bytes=64)
+            turn(w_bf[j], w_turned[j][:])
+
+        def quant_w(j):
+            h, part = divmod(j, 2)
+            if part == 0:
+                w_codes[h] = keep.tile([P, half], U32, name="w_codes%d" % h, align_bytes=64)
+                w_scales[h] = keep.tile([P, half], U8, name="w_scales%d" % h, align_bytes=64)
+            cols = slice(part * P, (part + 1) * P)
+            nc.vector.quantize_mx(w_codes[h][:, cols].bitcast(FP8X4), w_scales[h][:, cols], w_turned[j][:])
+
+        def pick_values(r, on_scalar):
+            tag = ("w_bf1", "w_bf3", "v_codes0", "v_bf3")[r]
+            v_bf[r] = keep.tile([P, I], BF16, name="v_bf%d" % r, tag=tag, align_bytes=64)
+            if on_scalar > 0:
+                nc.scalar.activation(
+                    v_bf[r][:, 0:on_scalar], vals_raw[r][:].indirect(key_list[:, 0 : on_scalar // 16]), COPY
+                )
+            if on_scalar < I:
+                nc.vector.tensor_copy(
+                    v_bf[r][:, on_scalar:I], vals_raw[r][:].indirect(key_list[:, on_scalar // 16 : I // 16])
+                )
+
+        def turn_v(r):
+            v_turned[r] = keep.tile([P, P * PACK], BF16, name="v_turned%d" % r, align_bytes=64)
+            turn(v_bf[r], v_turned[r][:])
+
+        def quant_v(r):
+            if r == 2:
+                v_codes[r] = late.tile([P, P], U32, name="v_codes2", align_bytes=64, offset=2048)
+            else:
+                v_codes[r] = keep.tile([P, P], U32, name="v_codes%d" % r, tag="v_codes%d" % r, align_bytes=64)
+            v_scales[r] = keep.tile([P, P], U8, name="v_scales%d" % r, align_bytes=64)
+            nc.vector.quantize_mx(v_codes[r][:].bitcast(FP8X4), v_scales[r][:], v_turned[r][:])
+
+        def read_out(r):
+            if r == 1:
+                o_whole[r] = late.tile([P, Q], F32, name="o_whole1", align_bytes=64, offset=0)
+            else:
+                o_whole[r] = keep.tile([P, Q], F32, name="o_whole%d" % r)
+            for h in range(2):
+                cols = slice(h * half, (h + 1) * half)
+                acc = psum.tile([P, half], F32, name="acc", tag="product", bufs=4)
+                nc.tensor.matmul_mx(
+                    acc[:],
+                    lhsT=v_codes[r][:].bitcast(FP8X4),
+                    lhsT_scale=v_scales[r][:],
+                    rhs=w_codes[h][:].bitcast(FP8X4),
+                    rhs_scale=w_scales[h][:],
+                    start=True,
+                    stop=True,
+                )
+                if r == PACK - 1 and h == 1:
+                    nc.vector.tensor_copy(o_whole[r][:, cols], acc[:])
+                else:
+                    nc.scalar.copy(o_whole[r][:, cols], acc[:])
+
+        def pick_out(r):
+            nc.vector.tensor_tensor(y[:, r, :], o_whole[r][:].indirect(out_list[:]), gain_rows[:], MULT)
+            nc.sync.dma_start(out_dealt[:, r, :], y[:, r, :])
+
+        nc.vector.tensor_copy(picked_words[:], key_words[:].indirect(key_list[:]))
+        os_rows = spread(os_cols, I, "os_rows")
+        pick_factor(0)
+
+        q_bf = keep.tile([P, Q * PACK], BF16, name="q_bf", tag="earl0", align_bytes=64)
+        for h in range(2):
+            cast = nc.scalar.copy if h == 0 else nc.vector.tensor_copy
+            cast(
+                q_bf[:, h * half * PACK : (h + 1) * half * PACK].rearrange("p (c i t) -> p c t i", i=4, t=PACK),
+                query_raw[:, :, h * half : (h + 1) * half].rearrange("p t (c i) -> p c t i", i=4),
+            )
+        nc.vector.tensor_copy(picked_bytes[:], key_bytes[:].indirect(key_list[:]))
+        for h in range(2):
+            cols = slice(h * half, (h + 1) * half)
+            nc.vector.quantize_mx(
+                q_codes[:, cols].bitcast(FP8X4), q_scales[:, cols], q_bf[:, h * half * PACK : (h + 1) * half * PACK]
+            )
+
+        pick_factor(1)
+        weigh(0)
+        weigh(1)
+        pick_factor(2)
+        pick_factor(3)
+        turn_w(0)
+        turn_w(1)
+        weigh(2)
+        weigh(3)
+        pick_values(0, I)
+        turn_w(2)
+        turn_w(3)
+        turn_v(0)
+        quant_w(0)
+        quant_w(1)
+        quant_w(2)
+        pick_values(1, I // 2)
+        quant_w(3)
+        quant_v(0)
+        gain_rows = spread(gain_cols, C, "gain_rows")
+        turn_v(1)
+        read_out(0)
+        pick_values(2, 0)
+        y = keep.tile([P, PACK, C], F32, name="y", tag="vals2", align_bytes=64)
+        quant_v(1)
+        pick_out(0)
+        turn_v(2)
+        pick_values(3, SCALAR_SLOTS)
+        read_out(1)
+        turn_v(3)
+        quant_v(2)
+        pick_out(1)
+        quant_v(3)
+        read_out(2)
+        pick_out(2)
+        read_out(3)
+        pick_out(3)
+
+        y_bf = keep.tile([P, C * PACK], BF16, name="y_bf", align_bytes=64)
+        nc.vector.tensor_copy(
+            y_bf[:].rearrange("p (c i r) -> p c r i", i=4, r=PACK),
+            y[:].rearrange("p r (c i) -> p c r i", i=4),
+        )
+        y_codes = keep.tile([P, C], U32, name="y_codes", align_bytes=64)
+        y_scales = keep.tile([P, C], U8, name="y_scales", align_bytes=64)
+        nc.vector.quantize_mx(y_codes[:].bitcast(FP8X4), y_scales[:], y_bf[:])
+        nc.sync.dma_start(out_1[0].rearrange("p c r -> p (c r)").bitcast(I32), y_codes[:].bitcast(I32))
+        for quad in range(4):
+            queue = nc.scalar if quad % 2 == 0 else nc.sync
+            queue.dma_start(
+                out_2[0][4 * quad : 4 * quad + 4, :].bitcast(I32),
+                y_scales[32 * quad : 32 * quad + 4, :].bitcast(I32),
+            )

@@ -19,7 +19,7 @@ COPY = mybir.ActivationFunctionType.Copy
 
 P = 128
 PACK = 4
-SCALAR_SLOTS = 192
+SCALAR_SLOTS = 256
 
 
 def tile_attend_earliertable_pickedout_lean_pl_kernel(
@@ -29,6 +29,7 @@ def tile_attend_earliertable_pickedout_lean_pl_kernel(
     with ExitStack() as ctx:
         keep = ctx.enter_context(tc.tile_pool(name="keep", bufs=1))
         late = ctx.enter_context(tc.tile_pool(name="late", bufs=1))
+        early = ctx.enter_context(tc.tile_pool(name="early", bufs=1))
         psum = ctx.enter_context(tc.psum_pool(name="psum", bufs=1))
 
         key_list = keep.tile([P, I // 16], U16, name="key_list")
@@ -36,7 +37,7 @@ def tile_attend_earliertable_pickedout_lean_pl_kernel(
         out_list = keep.tile([P, C // 16], U16, name="out_list")
         key_words = keep.tile([P, T], U16, name="key_words")
         key_bytes = keep.tile([P, T], U8, name="key_bytes")
-        query_raw = keep.tile([P, PACK, Q], F32, name="query_raw", tag="query")
+        query_raw = early.tile([P, PACK, Q], F32, name="query_raw", align_bytes=64, offset=0)
         os_cols = keep.tile([P, I // P], F32, name="os_cols")
         gain_cols = keep.tile([P, C // P], F32, name="gain_cols")
         earl_raw = [keep.tile([P, Z], F32, name="earl_raw%d" % j, tag="earl%d" % j, align_bytes=64) for j in range(Q // P)]
@@ -87,7 +88,7 @@ def tile_attend_earliertable_pickedout_lean_pl_kernel(
 
         half = Q // 2
         picked_words = keep.tile([P, I], U16, name="picked_words", align_bytes=64)
-        picked_bytes = keep.tile([P, I], U8, name="picked_bytes", align_bytes=64)
+        picked_bytes = early.tile([P, I], U8, name="picked_bytes", align_bytes=64, offset=2048)
         q_codes = keep.tile([P, Q], U32, name="q_codes", align_bytes=64)
         q_scales = keep.tile([P, Q], U8, name="q_scales", align_bytes=64)
         w_codes, w_scales = {}, {}
@@ -97,7 +98,10 @@ def tile_attend_earliertable_pickedout_lean_pl_kernel(
         def pick_factor(j):
             factor[j] = keep.tile([P, I], F32, name="factor%d" % j, tag="factor%d" % j, align_bytes=64)
             if j > 0:
-                picked = keep.tile([P, I], F32, name="earl_picked%d" % j, tag=("", "query", "picked2", "picked3")[j])
+                if j == 1:
+                    picked = early.tile([P, I], F32, name="earl_picked1", align_bytes=64, offset=0)
+                else:
+                    picked = keep.tile([P, I], F32, name="earl_picked%d" % j, tag="earl%d" % (j - 1), align_bytes=64)
                 nc.scalar.activation(picked[:], earl_raw[j][:].indirect(earl_list[:]), COPY)
                 nc.vector.tensor_tensor(factor[j][:], picked[:], os_rows[:], MULT)
             else:
@@ -119,7 +123,7 @@ def tile_attend_earliertable_pickedout_lean_pl_kernel(
             nc.vector.tensor_tensor(w_bf[j][:], score[:], factor[j][:], MULT)
 
         def turn_w(j):
-            tag = ("earl3", "w_turned1", "vals0", "w_turned3")[j]
+            tag = ("earl3", "w_turned1", "vals0", "vals1")[j]
             w_turned[j] = keep.tile([P, P * PACK], BF16, name="w_turned%d" % j, tag=tag, align_bytes=64)
             turn(w_bf[j], w_turned[j][:])
 
@@ -132,7 +136,7 @@ def tile_attend_earliertable_pickedout_lean_pl_kernel(
             nc.vector.quantize_mx(w_codes[h][:, cols].bitcast(FP8X4), w_scales[h][:, cols], w_turned[j][:])
 
         def pick_values(r, on_scalar):
-            tag = ("w_bf1", "w_bf3", "v_codes0", "v_bf3")[r]
+            tag = ("w_bf1", "w_bf1", "v_turned1", "vals2")[r]
             v_bf[r] = keep.tile([P, I], BF16, name="v_bf%d" % r, tag=tag, align_bytes=64)
             if on_scalar > 0:
                 nc.scalar.activation(
@@ -144,22 +148,19 @@ def tile_attend_earliertable_pickedout_lean_pl_kernel(
                 )
 
         def turn_v(r):
-            v_turned[r] = keep.tile([P, P * PACK], BF16, name="v_turned%d" % r, align_bytes=64)
+            if r == 2:
+                v_turned[r] = late.tile([P, P * PACK], BF16, name="v_turned2", align_bytes=64, offset=4096)
+            else:
+                v_turned[r] = keep.tile([P, P * PACK], BF16, name="v_turned%d" % r, tag="v_turned%d" % r, align_bytes=64)
             turn(v_bf[r], v_turned[r][:])
 
         def quant_v(r):
-            if r == 2:
-                v_codes[r] = late.tile([P, P], U32, name="v_codes2", align_bytes=64, offset=2048)
-            else:
-                v_codes[r] = keep.tile([P, P], U32, name="v_codes%d" % r, tag="v_codes%d" % r, align_bytes=64)
+            v_codes[r] = keep.tile([P, P], U32, name="v_codes%d" % r, align_bytes=64)
             v_scales[r] = keep.tile([P, P], U8, name="v_scales%d" % r, align_bytes=64)
             nc.vector.quantize_mx(v_codes[r][:].bitcast(FP8X4), v_scales[r][:], v_turned[r][:])
 
         def read_out(r):
-            if r == 1:
-                o_whole[r] = late.tile([P, Q], F32, name="o_whole1", align_bytes=64, offset=0)
-            else:
-                o_whole[r] = keep.tile([P, Q], F32, name="o_whole%d" % r)
+            o_whole[r] = keep.tile([P, Q], F32, name="o_whole%d" % r)
             for h in range(2):
                 cols = slice(h * half, (h + 1) * half)
                 acc = psum.tile([P, half], F32, name="acc", tag="product", bufs=4)
@@ -210,41 +211,57 @@ def tile_attend_earliertable_pickedout_lean_pl_kernel(
         weigh(3)
         pick_values(0, I)
         turn_w(2)
-        turn_w(3)
         turn_v(0)
         quant_w(0)
         quant_w(1)
-        quant_w(2)
-        pick_values(1, I // 2)
-        quant_w(3)
-        quant_v(0)
-        gain_rows = spread(gain_cols, C, "gain_rows")
+        pick_values(1, SCALAR_SLOTS)
+        turn_w(3)
         turn_v(1)
+        gain_rows = spread(gain_cols, C, "gain_rows")
+        quant_w(2)
+        quant_v(0)
+        quant_w(3)
         read_out(0)
-        pick_values(2, 0)
-        y = keep.tile([P, PACK, C], F32, name="y", tag="vals2", align_bytes=64)
         quant_v(1)
-        pick_out(0)
-        turn_v(2)
-        pick_values(3, SCALAR_SLOTS)
+        pick_values(2, 0)
         read_out(1)
+        pick_values(3, SCALAR_SLOTS)
+        turn_v(2)
         turn_v(3)
+        y = late.tile([P, PACK, C], F32, name="y", align_bytes=64, offset=0)
+        pick_out(0)
         quant_v(2)
         pick_out(1)
         quant_v(3)
         read_out(2)
         pick_out(2)
         read_out(3)
-        pick_out(3)
 
+        hc = C // 2
+        last = PACK - 1
         y_bf = keep.tile([P, C * PACK], BF16, name="y_bf", align_bytes=64)
-        nc.vector.tensor_copy(
-            y_bf[:].rearrange("p (c i r) -> p c r i", i=4, r=PACK),
-            y[:].rearrange("p r (c i) -> p c r i", i=4),
-        )
         y_codes = keep.tile([P, C], U32, name="y_codes", align_bytes=64)
         y_scales = keep.tile([P, C], U8, name="y_scales", align_bytes=64)
-        nc.vector.quantize_mx(y_codes[:].bitcast(FP8X4), y_scales[:], y_bf[:])
+        for h in range(2):
+            cols = slice(h * hc, (h + 1) * hc)
+            nc.vector.tensor_tensor(
+                y[:, last, cols],
+                o_whole[last][:].indirect(out_list[:, h * hc // 16 : (h + 1) * hc // 16]),
+                gain_rows[:, cols],
+                MULT,
+            )
+        nc.sync.dma_start(out_dealt[:, last, :], y[:, last, :])
+        for h in range(2):
+            cast = nc.scalar.copy if h == 0 else nc.vector.tensor_copy
+            cast(
+                y_bf[:, h * hc * PACK : (h + 1) * hc * PACK].rearrange("p (c i r) -> p c r i", i=4, r=PACK),
+                y[:, :, h * hc : (h + 1) * hc].rearrange("p r (c i) -> p c r i", i=4),
+            )
+        for h in range(2):
+            cols = slice(h * hc, (h + 1) * hc)
+            nc.vector.quantize_mx(
+                y_codes[:, cols].bitcast(FP8X4), y_scales[:, cols], y_bf[:, h * hc * PACK : (h + 1) * hc * PACK]
+            )
         nc.sync.dma_start(out_1[0].rearrange("p c r -> p (c r)").bitcast(I32), y_codes[:].bitcast(I32))
         for quad in range(4):
             queue = nc.scalar if quad % 2 == 0 else nc.sync

@@ -30,6 +30,8 @@ def tile_attend_earliertable_pickedout_lean_pl_kernel(
         keep = ctx.enter_context(tc.tile_pool(name="keep", bufs=1))
         late = ctx.enter_context(tc.tile_pool(name="late", bufs=1))
         early = ctx.enter_context(tc.tile_pool(name="early", bufs=1))
+        first = ctx.enter_context(tc.tile_pool(name="first", bufs=1))
+        second = ctx.enter_context(tc.tile_pool(name="second", bufs=1))
         psum = ctx.enter_context(tc.psum_pool(name="psum", bufs=1))
 
         key_list = keep.tile([P, I // 16], U16, name="key_list")
@@ -41,8 +43,12 @@ def tile_attend_earliertable_pickedout_lean_pl_kernel(
         os_cols = keep.tile([P, I // P], F32, name="os_cols")
         gain_cols = keep.tile([P, C // P], F32, name="gain_cols")
         earl_raw = [keep.tile([P, Z], F32, name="earl_raw%d" % j, tag="earl%d" % j, align_bytes=64) for j in range(Q // P)]
-        vals_raw = [keep.tile([P, T], F32, name="vals_raw%d" % r, tag="vals%d" % r, align_bytes=64) for r in range(PACK - 1)]
-        vals_raw.append(late.tile([P, T], F32, name="vals_raw3", align_bytes=64, offset=0))
+        vals_raw = [
+            first.tile([P, T], F32, name="vals_raw0", align_bytes=64, offset=0),
+            second.tile([P, T], F32, name="vals_raw1", align_bytes=64, offset=0),
+            keep.tile([P, T], F32, name="vals_raw2", tag="vals2", align_bytes=64),
+            late.tile([P, T], F32, name="vals_raw3", align_bytes=64, offset=0),
+        ]
         ident = keep.tile([P, P], F32, name="ident")
 
         nc.gpsimd.memset(key_bytes[:].bitcast(I32), 0)
@@ -96,7 +102,7 @@ def tile_attend_earliertable_pickedout_lean_pl_kernel(
         factor, w_bf, w_turned, v_bf, v_turned, v_codes, v_scales, o_whole = {}, {}, {}, {}, {}, {}, {}, {}
 
         def pick_factor(j):
-            factor[j] = keep.tile([P, I], F32, name="factor%d" % j, tag="factor%d" % j, align_bytes=64)
+            factor[j] = keep.tile([P, I], F32, name="factor%d" % j, tag="factor%d" % (j % 2), align_bytes=64)
             if j > 0:
                 if j == 1:
                     picked = early.tile([P, I], F32, name="earl_picked1", align_bytes=64, offset=0)
@@ -119,12 +125,18 @@ def tile_attend_earliertable_pickedout_lean_pl_kernel(
                 start=True,
                 stop=True,
             )
-            w_bf[j] = keep.tile([P, I], BF16, name="w_bf%d" % j, tag="w_bf%d" % j, align_bytes=64)
+            if j == 2:
+                w_bf[j] = first.tile([P, I], BF16, name="w_bf2", align_bytes=64, offset=0)
+            else:
+                w_bf[j] = keep.tile([P, I], BF16, name="w_bf%d" % j, align_bytes=64)
             nc.vector.tensor_tensor(w_bf[j][:], score[:], factor[j][:], MULT)
 
         def turn_w(j):
-            tag = ("earl3", "w_turned1", "vals0", "vals1")[j]
-            w_turned[j] = keep.tile([P, P * PACK], BF16, name="w_turned%d" % j, tag=tag, align_bytes=64)
+            if j == 0:
+                w_turned[j] = keep.tile([P, P * PACK], BF16, name="w_turned0", align_bytes=64)
+            else:
+                home = first if j == 1 else second
+                w_turned[j] = home.tile([P, P * PACK], BF16, name="w_turned%d" % j, align_bytes=64, offset=1024 * j)
             turn(w_bf[j], w_turned[j][:])
 
         def quant_w(j):
@@ -136,7 +148,7 @@ def tile_attend_earliertable_pickedout_lean_pl_kernel(
             nc.vector.quantize_mx(w_codes[h][:, cols].bitcast(FP8X4), w_scales[h][:, cols], w_turned[j][:])
 
         def pick_values(r, on_scalar):
-            tag = ("w_bf1", "w_bf1", "v_turned1", "vals2")[r]
+            tag = ("earl3", "factor1", "v_turned1", "vals2")[r]
             v_bf[r] = keep.tile([P, I], BF16, name="v_bf%d" % r, tag=tag, align_bytes=64)
             if on_scalar > 0:
                 nc.scalar.activation(
@@ -155,12 +167,18 @@ def tile_attend_earliertable_pickedout_lean_pl_kernel(
             turn(v_bf[r], v_turned[r][:])
 
         def quant_v(r):
-            v_codes[r] = keep.tile([P, P], U32, name="v_codes%d" % r, align_bytes=64)
+            if r == 0:
+                v_codes[r] = second.tile([P, P], U32, name="v_codes0", align_bytes=64, offset=0)
+            else:
+                v_codes[r] = keep.tile([P, P], U32, name="v_codes%d" % r, align_bytes=64)
             v_scales[r] = keep.tile([P, P], U8, name="v_scales%d" % r, align_bytes=64)
             nc.vector.quantize_mx(v_codes[r][:].bitcast(FP8X4), v_scales[r][:], v_turned[r][:])
 
         def read_out(r):
-            o_whole[r] = keep.tile([P, Q], F32, name="o_whole%d" % r)
+            if r == 1:
+                o_whole[r] = late.tile([P, Q], F32, name="o_whole1", align_bytes=64, offset=6144)
+            else:
+                o_whole[r] = keep.tile([P, Q], F32, name="o_whole%d" % r)
             for h in range(2):
                 cols = slice(h * half, (h + 1) * half)
                 acc = psum.tile([P, half], F32, name="acc", tag="product", bufs=4)
@@ -173,10 +191,7 @@ def tile_attend_earliertable_pickedout_lean_pl_kernel(
                     start=True,
                     stop=True,
                 )
-                if r == PACK - 1 and h == 1:
-                    nc.vector.tensor_copy(o_whole[r][:, cols], acc[:])
-                else:
-                    nc.scalar.copy(o_whole[r][:, cols], acc[:])
+                nc.scalar.copy(o_whole[r][:, cols], acc[:])
 
         def pick_out(r):
             nc.vector.tensor_tensor(y[:, r, :], o_whole[r][:].indirect(out_list[:]), gain_rows[:], MULT)
@@ -202,31 +217,31 @@ def tile_attend_earliertable_pickedout_lean_pl_kernel(
 
         pick_factor(1)
         weigh(0)
-        weigh(1)
         pick_factor(2)
+        weigh(1)
         pick_factor(3)
         turn_w(0)
+        pick_values(0, I)
         turn_w(1)
+        quant_w(0)
         weigh(2)
         weigh(3)
-        pick_values(0, I)
-        turn_w(2)
         turn_v(0)
-        quant_w(0)
         quant_w(1)
         pick_values(1, SCALAR_SLOTS)
+        turn_w(2)
         turn_w(3)
         turn_v(1)
         gain_rows = spread(gain_cols, C, "gain_rows")
-        quant_w(2)
         quant_v(0)
+        quant_w(2)
         quant_w(3)
         read_out(0)
         quant_v(1)
         pick_values(2, 0)
-        read_out(1)
         pick_values(3, SCALAR_SLOTS)
         turn_v(2)
+        read_out(1)
         turn_v(3)
         y = late.tile([P, PACK, C], F32, name="y", align_bytes=64, offset=0)
         pick_out(0)

@@ -32,6 +32,7 @@ def tile_attend_earliertable_pickedout_lean_pl_kernel(
         early = ctx.enter_context(tc.tile_pool(name="early", bufs=1))
         first = ctx.enter_context(tc.tile_pool(name="first", bufs=1))
         second = ctx.enter_context(tc.tile_pool(name="second", bufs=1))
+        tables = ctx.enter_context(tc.tile_pool(name="tables", bufs=1))
         psum = ctx.enter_context(tc.psum_pool(name="psum", bufs=1))
 
         key_list = keep.tile([P, I // 16], U16, name="key_list")
@@ -40,9 +41,14 @@ def tile_attend_earliertable_pickedout_lean_pl_kernel(
         key_words = keep.tile([P, T], U16, name="key_words")
         key_bytes = keep.tile([P, T], U8, name="key_bytes")
         query_raw = early.tile([P, PACK, Q], F32, name="query_raw", align_bytes=64, offset=0)
-        os_cols = keep.tile([P, I // P], F32, name="os_cols")
+        os_cols = keep.tile([P, I // P], F32, name="os_cols", tag="earl_picked1", align_bytes=64)
         gain_cols = keep.tile([P, C // P], F32, name="gain_cols")
-        earl_raw = [keep.tile([P, Z], F32, name="earl_raw%d" % j, tag="earl%d" % j, align_bytes=64) for j in range(Q // P)]
+        earl_raw = [
+            tables.tile([P, Z], F32, name="earl_raw0", align_bytes=64, offset=0),
+            tables.tile([P, Z], F32, name="earl_raw1", align_bytes=64, offset=4096),
+            keep.tile([P, Z], F32, name="earl_raw2", tag="earl2", align_bytes=64),
+            keep.tile([P, Z], F32, name="earl_raw3", tag="earl3", align_bytes=64),
+        ]
         vals_raw = [
             first.tile([P, T], F32, name="vals_raw0", align_bytes=64, offset=0),
             second.tile([P, T], F32, name="vals_raw1", align_bytes=64, offset=0),
@@ -58,13 +64,14 @@ def tile_attend_earliertable_pickedout_lean_pl_kernel(
         nc.sync.dma_start(os_cols[:], slot_factor.rearrange("o (n m) -> (o n) m", n=P))
         nc.sync.dma_start(earl_list[:], offs2)
         nc.sync.dma_start(earl_raw[0][:], earl[0:P, :])
+        nc.sync.dma_start(earl_raw[1][:], earl[P : 2 * P, :])
         nc.sync.dma_start(query_raw[:], query.rearrange("(p t) q -> p t q", t=PACK))
         for quad in range(4):
             nc.sync.dma_start(
                 key_bytes[32 * quad : 32 * quad + 4, :].bitcast(I32),
                 keys_scales[0][4 * quad : 4 * quad + 4, :].bitcast(I32),
             )
-        for j in range(1, Q // P):
+        for j in range(2, Q // P):
             nc.sync.dma_start(earl_raw[j][:], earl[j * P : (j + 1) * P, :])
         nc.sync.dma_start(vals_raw[0][:], vals_dealt[0])
         nc.sync.dma_start(gain_cols[:], pgain.rearrange("o (n m) -> (o n) m", n=P))
@@ -102,12 +109,13 @@ def tile_attend_earliertable_pickedout_lean_pl_kernel(
         factor, w_bf, w_turned, v_bf, v_turned, v_codes, v_scales, o_whole = {}, {}, {}, {}, {}, {}, {}, {}
 
         def pick_factor(j):
-            factor[j] = keep.tile([P, I], F32, name="factor%d" % j, tag="factor%d" % (j % 2), align_bytes=64)
+            factor[j] = keep.tile([P, I], F32, name="factor%d" % j, tag="factor%d" % (1 if j == 3 else j), align_bytes=64)
             if j > 0:
-                if j == 1:
-                    picked = early.tile([P, I], F32, name="earl_picked1", align_bytes=64, offset=0)
+                if j == 2:
+                    picked = early.tile([P, I], F32, name="earl_picked2", align_bytes=64, offset=0)
                 else:
-                    picked = keep.tile([P, I], F32, name="earl_picked%d" % j, tag="earl%d" % (j - 1), align_bytes=64)
+                    tag = "earl2" if j == 3 else "earl_picked1"
+                    picked = keep.tile([P, I], F32, name="earl_picked%d" % j, tag=tag, align_bytes=64)
                 nc.scalar.activation(picked[:], earl_raw[j][:].indirect(earl_list[:]), COPY)
                 nc.vector.tensor_tensor(factor[j][:], picked[:], os_rows[:], MULT)
             else:
@@ -132,11 +140,8 @@ def tile_attend_earliertable_pickedout_lean_pl_kernel(
             nc.vector.tensor_tensor(w_bf[j][:], score[:], factor[j][:], MULT)
 
         def turn_w(j):
-            if j == 0:
-                w_turned[j] = keep.tile([P, P * PACK], BF16, name="w_turned0", align_bytes=64)
-            else:
-                home = first if j == 1 else second
-                w_turned[j] = home.tile([P, P * PACK], BF16, name="w_turned%d" % j, align_bytes=64, offset=1024 * j)
+            home = first if j < 2 else second
+            w_turned[j] = home.tile([P, P * PACK], BF16, name="w_turned%d" % j, align_bytes=64, offset=1024 * (j + 1))
             turn(w_bf[j], w_turned[j][:])
 
         def quant_w(j):
@@ -176,7 +181,7 @@ def tile_attend_earliertable_pickedout_lean_pl_kernel(
 
         def read_out(r):
             if r == 1:
-                o_whole[r] = late.tile([P, Q], F32, name="o_whole1", align_bytes=64, offset=6144)
+                o_whole[r] = keep.tile([P, Q], F32, name="o_whole1", tag="vals2", align_bytes=64)
             else:
                 o_whole[r] = keep.tile([P, Q], F32, name="o_whole%d" % r)
             for h in range(2):
@@ -200,35 +205,35 @@ def tile_attend_earliertable_pickedout_lean_pl_kernel(
         nc.vector.tensor_copy(picked_words[:], key_words[:].indirect(key_list[:]))
         os_rows = spread(os_cols, I, "os_rows")
         pick_factor(0)
+        pick_factor(1)
 
-        q_bf = keep.tile([P, Q * PACK], BF16, name="q_bf", tag="earl0", align_bytes=64)
+        q_bf = tables.tile([P, Q * PACK], BF16, name="q_bf", align_bytes=64, offset=2048)
         for h in range(2):
             cast = nc.scalar.copy if h == 0 else nc.vector.tensor_copy
             cast(
                 q_bf[:, h * half * PACK : (h + 1) * half * PACK].rearrange("p (c i t) -> p c t i", i=4, t=PACK),
                 query_raw[:, :, h * half : (h + 1) * half].rearrange("p t (c i) -> p c t i", i=4),
             )
-        nc.vector.tensor_copy(picked_bytes[:], key_bytes[:].indirect(key_list[:]))
         for h in range(2):
             cols = slice(h * half, (h + 1) * half)
             nc.vector.quantize_mx(
                 q_codes[:, cols].bitcast(FP8X4), q_scales[:, cols], q_bf[:, h * half * PACK : (h + 1) * half * PACK]
             )
 
-        pick_factor(1)
-        weigh(0)
+        nc.vector.tensor_copy(picked_bytes[:], key_bytes[:].indirect(key_list[:]))
         pick_factor(2)
+        weigh(0)
         weigh(1)
         pick_factor(3)
-        turn_w(0)
         pick_values(0, I)
+        turn_w(0)
         turn_w(1)
-        quant_w(0)
         weigh(2)
         weigh(3)
         turn_v(0)
-        quant_w(1)
         pick_values(1, SCALAR_SLOTS)
+        quant_w(0)
+        quant_w(1)
         turn_w(2)
         turn_w(3)
         turn_v(1)
@@ -241,13 +246,13 @@ def tile_attend_earliertable_pickedout_lean_pl_kernel(
         pick_values(2, 0)
         pick_values(3, SCALAR_SLOTS)
         turn_v(2)
-        read_out(1)
         turn_v(3)
         y = late.tile([P, PACK, C], F32, name="y", align_bytes=64, offset=0)
         pick_out(0)
         quant_v(2)
-        pick_out(1)
         quant_v(3)
+        read_out(1)
+        pick_out(1)
         read_out(2)
         pick_out(2)
         read_out(3)

from contextlib import ExitStack

import concourse.mybir as mybir
from concourse.masks import make_identity

D, T, I, Q, E, Z, C = 512, 2048, 512, 512, 512, 1024, 256
FLOPS = 2 * D * Q * I + 2 * I * E * Q

F32 = mybir.dt.float32
BF16 = mybir.dt.bfloat16
I32 = mybir.dt.int32
U32 = mybir.dt.uint32
U16 = mybir.dt.uint16
U8 = mybir.dt.uint8
FP8X4 = mybir.dt.float8_e4m3fn_x4
FP4X4 = mybir.dt.float4_e2m1fn_x4
MULT = mybir.AluOpType.mult
COPY = mybir.ActivationFunctionType.Copy

P = 128
PACK = 4
SCALAR_SLOTS = 256


def tile_attend_earliertable_pickedout_lean_pl_kernel(
    tc, query, keys_words, keys_scales, earl, slot_factor, vals, pgain, offs, offs2, offs3, out_0, out_1, out_2
):
    nc = tc.nc
    with ExitStack() as ctx:
        keep = ctx.enter_context(tc.tile_pool(name="keep", bufs=1))
        late = ctx.enter_context(tc.tile_pool(name="late", bufs=1))
        early = ctx.enter_context(tc.tile_pool(name="early", bufs=1))
        first = ctx.enter_context(tc.tile_pool(name="first", bufs=1))
        second = ctx.enter_context(tc.tile_pool(name="second", bufs=1))
        tables = ctx.enter_context(tc.tile_pool(name="tables", bufs=1))
        psum = ctx.enter_context(tc.psum_pool(name="psum", bufs=1))

        key_list = keep.tile([P, I // 16], U16, name="key_list")
        earl_list = keep.tile([P, I // 16], U16, name="earl_list")
        out_list = keep.tile([P, C // 16], U16, name="out_list")
        key_words = keep.tile([P, T], U16, name="key_words")
        key_bytes = keep.tile([P, T], U8, name="key_bytes")
        query_raw = early.tile([P, PACK, Q], F32, name="query_raw", align_bytes=64, offset=0)
        os_cols = keep.tile([P, I // P], F32, name="os_cols", tag="earl_picked1", align_bytes=64)
        gain_cols = keep.tile([P, C // P], F32, name="gain_cols")
        earl_raw = [
            tables.tile([P, Z], F32, name="earl_raw0", align_bytes=64, offset=0),
            tables.tile([P, Z], F32, name="earl_raw1", align_bytes=64, offset=4096),
            keep.tile([P, Z], F32, name="earl_raw2", tag="earl2", align_bytes=64),
            keep.tile([P, Z], F32, name="earl_raw3", tag="earl3", align_bytes=64),
        ]
        vals_raw = [
            first.tile([P, T], F32, name="vals_raw0", align_bytes=64, offset=0),
            second.tile([P, T], F32, name="vals_raw1", align_bytes=64, offset=0),
            keep.tile([P, T], F32, name="vals_raw2", tag="vals2", align_bytes=64),
            late.tile([P, T], F32, name="vals_raw3", align_bytes=64, offset=0),
        ]
        ident = keep.tile([P, P], F32, name="ident")

        nc.gpsimd.memset(key_bytes[:].bitcast(I32), 0)
        vals_dealt = vals.rearrange("(p r) t -> r p t", r=PACK)
        nc.sync.dma_start(key_words[:].bitcast(I32), keys_words[0].bitcast(I32))
        nc.sync.dma_start(key_list[:], offs)
        nc.sync.dma_start(os_cols[:], slot_factor.rearrange("o (n m) -> (o n) m", n=P))
        nc.sync.dma_start(earl_list[:], offs2)
        nc.sync.dma_start(earl_raw[0][:], earl[0:P, :])
        nc.sync.dma_start(earl_raw[1][:], earl[P : 2 * P, :])
        nc.sync.dma_start(query_raw[:], query.rearrange("(p t) q -> p t q", t=PACK))
        for quad in range(4):
            nc.sync.dma_start(
                key_bytes[32 * quad : 32 * quad + 4, :].bitcast(I32),
                keys_scales[0][4 * quad : 4 * quad + 4, :].bitcast(I32),
            )
        for j in range(2, Q // P):
            nc.sync.dma_start(earl_raw[j][:], earl[j * P : (j + 1) * P, :])
        nc.sync.dma_start(vals_raw[0][:], vals_dealt[0])
        nc.sync.dma_start(gain_cols[:], pgain.rearrange("o (n m) -> (o n) m", n=P))
        nc.sync.dma_start(out_list[:], offs3)
        for r in range(1, PACK):
            nc.sync.dma_start(vals_raw[r][:], vals_dealt[r])

        make_identity(nc, ident[:])

        def spread(cols, width, name):
            per = width // P
            bank = psum.tile([P, per, P], F32, name=name + "_bank", tag="turn", bufs=4)
            for m in range(per):
                nc.tensor.transpose(bank[:, m, :], cols[:, m : m + 1].to_broadcast([P, P]), ident[:])
            rows = keep.tile([P, width], F32, name=name)
            nc.scalar.copy(rows[:].rearrange("p (n m) -> p n m", m=per), bank[:].rearrange("p m n -> p n m"))
            return rows

        def turn(src, dst):
            words = src[:].bitcast(F32)
            bank = psum.tile([P, 2, P], F32, name="turn_bank", tag="turn", bufs=4)
            for u in range(2):
                nc.tensor.transpose(bank[:, u, :], words[:, u : 2 * P : 2], ident[:])
            nc.scalar.copy(
                dst.bitcast(F32).rearrange("p (x u) -> p x u", u=2), bank[:].rearrange("p u x -> p x u")
            )

        half = Q // 2
        picked_words = keep.tile([P, I], U16, name="picked_words", align_bytes=64)
        picked_bytes = early.tile([P, I], U8, name="picked_bytes", align_bytes=64, offset=2048)
        q_codes = keep.tile([P, Q], U32, name="q_codes", align_bytes=64)
        q_scales = keep.tile([P, Q], U8, name="q_scales", align_bytes=64)
        w_codes, w_scales = {}, {}
        out_dealt = out_0.rearrange("(p r) c -> p r c", r=PACK)
        factor, w_bf, w_turned, v_bf, v_turned, v_codes, v_scales, o_whole = {}, {}, {}, {}, {}, {}, {}, {}

        def pick_factor(j):
            factor[j] = keep.tile([P, I], F32, name="factor%d" % j, tag="factor%d" % (1 if j == 3 else j), align_bytes=64)
            if j > 0:
                if j == 2:
                    picked = early.tile([P, I], F32, name="earl_picked2", align_bytes=64, offset=0)
                else:
                    tag = "earl2" if j == 3 else "earl_picked1"
                    picked = keep.tile([P, I], F32, name="earl_picked%d" % j, tag=tag, align_bytes=64)
                nc.scalar.activation(picked[:], earl_raw[j][:].indirect(earl_list[:]), COPY)
                nc.vector.tensor_tensor(factor[j][:], picked[:], os_rows[:], MULT)
            else:
                nc.vector.tensor_tensor(factor[j][:], earl_raw[j][:].indirect(earl_list[:]), os_rows[:], MULT)

        def weigh(j):
            cols = slice(j * P, (j + 1) * P)
            score = psum.tile([P, I], F32, name="score", tag="product", bufs=4)
            nc.tensor.matmul_mx(
                score[:],
                lhsT=q_codes[:, cols].bitcast(FP8X4),
                lhsT_scale=q_scales[:, cols],
                rhs=picked_words[:].bitcast(FP4X4),
                rhs_scale=picked_bytes[:],
                start=True,
                stop=True,
            )
            if j == 2:
                w_bf[j] = first.tile([P, I], BF16, name="w_bf2", align_bytes=64, offset=0)
            else:
                w_bf[j] = keep.tile([P, I], BF16, name="w_bf%d" % j, align_bytes=64)
            nc.vector.tensor_tensor(w_bf[j][:], score[:], factor[j][:], MULT)

        def turn_w(j):
            home = first if j < 2 else second
            w_turned[j] = home.tile([P, P * PACK], BF16, name="w_turned%d" % j, align_bytes=64, offset=1024 * (j + 1))
            turn(w_bf[j], w_turned[j][:])

        def quant_w(j):
            h, part = divmod(j, 2)
            if part == 0:
                w_codes[h] = keep.tile([P, half], U32, name="w_codes%d" % h, align_bytes=64)
                w_scales[h] = keep.tile([P, half], U8, name="w_scales%d" % h, align_bytes=64)
            cols = slice(part * P, (part + 1) * P)
            nc.vector.quantize_mx(w_codes[h][:, cols].bitcast(FP8X4), w_scales[h][:, cols], w_turned[j][:])

        def pick_values(r, on_scalar):
            tag = ("earl3", "factor1", "v_turned1", "vals2")[r]
            v_bf[r] = keep.tile([P, I], BF16, name="v_bf%d" % r, tag=tag, align_bytes=64)
            if on_scalar > 0:
                nc.scalar.activation(
                    v_bf[r][:, 0:on_scalar], vals_raw[r][:].indirect(key_list[:, 0 : on_scalar // 16]), COPY
                )
            if on_scalar < I:
                nc.vector.tensor_copy(
                    v_bf[r][:, on_scalar:I], vals_raw[r][:].indirect(key_list[:, on_scalar // 16 : I // 16])
                )

        def turn_v(r):
            if r == 2:
                v_turned[r] = late.tile([P, P * PACK], BF16, name="v_turned2", align_bytes=64, offset=4096)
            else:
                v_turned[r] = keep.tile([P, P * PACK], BF16, name="v_turned%d" % r, tag="v_turned%d" % r, align_bytes=64)
            turn(v_bf[r], v_turned[r][:])

        def quant_v(r):
            if r == 0:
                v_codes[r] = second.tile([P, P], U32, name="v_codes0", align_bytes=64, offset=0)
            else:
                v_codes[r] = keep.tile([P, P], U32, name="v_codes%d" % r, align_bytes=64)
            v_scales[r] = keep.tile([P, P], U8, name="v_scales%d" % r, align_bytes=64)
            nc.vector.quantize_mx(v_codes[r][:].bitcast(FP8X4), v_scales[r][:], v_turned[r][:])

        def read_out(r):
            if r == 1:
                o_whole[r] = keep.tile([P, Q], F32, name="o_whole1", tag="vals2", align_bytes=64)
            else:
                o_whole[r] = keep.tile([P, Q], F32, name="o_whole%d" % r)
            for h in range(2):
                cols = slice(h * half, (h + 1) * half)
                acc = psum.tile([P, half], F32, name="acc", tag="product", bufs=4)
                nc.tensor.matmul_mx(
                    acc[:],
                    lhsT=v_codes[r][:].bitcast(FP8X4),
                    lhsT_scale=v_scales[r][:],
                    rhs=w_codes[h][:].bitcast(FP8X4),
                    rhs_scale=w_scales[h][:],
                    start=True,
                    stop=True,
                )
                nc.scalar.copy(o_whole[r][:, cols], acc[:])

        def pick_out(r):
            nc.vector.tensor_tensor(y[:, r, :], o_whole[r][:].indirect(out_list[:]), gain_rows[:], MULT)
            nc.sync.dma_start(out_dealt[:, r, :], y[:, r, :])

        nc.vector.tensor_copy(picked_words[:], key_words[:].indirect(key_list[:]))
        os_rows = spread(os_cols, I, "os_rows")
        pick_factor(0)
        pick_factor(1)

        q_bf = tables.tile([P, Q * PACK], BF16, name="q_bf", align_bytes=64, offset=2048)
        for h in range(2):
            cast = nc.scalar.copy if h == 0 else nc.vector.tensor_copy
            cast(
                q_bf[:, h * half * PACK : (h + 1) * half * PACK].rearrange("p (c i t) -> p c t i", i=4, t=PACK),
                query_raw[:, :, h * half : (h + 1) * half].rearrange("p t (c i) -> p c t i", i=4),
            )
        for h in range(2):
            cols = slice(h * half, (h + 1) * half)
            nc.vector.quantize_mx(
                q_codes[:, cols].bitcast(FP8X4), q_scales[:, cols], q_bf[:, h * half * PACK : (h + 1) * half * PACK]
            )

        nc.vector.tensor_copy(picked_bytes[:], key_bytes[:].indirect(key_list[:]))
        pick_factor(2)
        weigh(0)
        weigh(1)
        pick_factor(3)
        pick_values(0, I)
        turn_w(0)
        turn_w(1)
        weigh(2)
        weigh(3)
        turn_v(0)
        pick_values(1, SCALAR_SLOTS)
        quant_w(0)
        quant_w(1)
        turn_w(2)
        turn_w(3)
        turn_v(1)
        gain_rows = spread(gain_cols, C, "gain_rows")
        quant_v(0)
        quant_w(2)
        quant_w(3)
        read_out(0)
        quant_v(1)
        pick_values(2, 0)
        pick_values(3, SCALAR_SLOTS)
        turn_v(2)
        turn_v(3)
        y = late.tile([P, PACK, C], F32, name="y", align_bytes=64, offset=0)
        pick_out(0)
        quant_v(2)
        quant_v(3)
        read_out(1)
        pick_out(1)
        read_out(2)
        pick_out(2)
        read_out(3)

        hc = C // 2
        last = PACK - 1
        y_bf = keep.tile([P, C * PACK], BF16, name="y_bf", align_bytes=64)
        y_codes = keep.tile([P, C], U32, name="y_codes", align_bytes=64)
        y_scales = keep.tile([P, C], U8, name="y_scales", align_bytes=64)
        for h in range(2):
            cols = slice(h * hc, (h + 1) * hc)
            nc.vector.tensor_tensor(
                y[:, last, cols],
                o_whole[last][:].indirect(out_list[:, h * hc // 16 : (h + 1) * hc // 16]),
                gain_rows[:, cols],
                MULT,
            )
        nc.sync.dma_start(out_dealt[:, last, :], y[:, last, :])
        for h in range(2):
            cast = nc.scalar.copy if h == 0 else nc.vector.tensor_copy
            cast(
                y_bf[:, h * hc * PACK : (h + 1) * hc * PACK].rearrange("p (c i r) -> p c r i", i=4, r=PACK),
                y[:, :, h * hc : (h + 1) * hc].rearrange("p r (c i) -> p c r i", i=4),
            )
        for h in range(2):
            cols = slice(h * hc, (h + 1) * hc)
            nc.vector.quantize_mx(
                y_codes[:, cols].bitcast(FP8X4), y_scales[:, cols], y_bf[:, h * hc * PACK : (h + 1) * hc * PACK]
            )
        nc.sync.dma_start(out_1[0].rearrange("p c r -> p (c r)").bitcast(I32), y_codes[:].bitcast(I32))
        for quad in range(4):
            queue = nc.scalar if quad % 2 == 0 else nc.sync
            queue.dma_start(
                out_2[0][4 * quad : 4 * quad + 4, :].bitcast(I32),
                y_scales[32 * quad : 32 * quad + 4, :].bitcast(I32),
            )
